import numpy as np
import ml_dtypes


def mxq(x, axis, fmt="e4m3"):
    dtype, down = {"e4m3": (ml_dtypes.float8_e4m3fn, 7), "e5m2": (ml_dtypes.float8_e5m2, 14)}[fmt]
    v = np.moveaxis(np.asarray(x, np.float32).astype(ml_dtypes.bfloat16).astype(np.float64), axis, -1)
    blocks = v.reshape(v.shape[:-1] + (-1, 32))
    amax = np.abs(blocks).max(-1, keepdims=True)
    byte = np.maximum(np.where(amax > 0, np.frexp(amax)[1] - 1 + 127, 0) - down, 1)
    scale = np.exp2(byte - 127.0)
    codes = (blocks / scale).astype(np.float32).astype(dtype).astype(np.float64)
    return np.moveaxis((codes * scale).reshape(v.shape), -1, axis)


WIDE = False


def mx_kscale(k):
    if not WIDE:
        return np.ones(k)
    levels = np.array([10, -10, 5, -5, 0])
    if k % 512:
        return np.exp2(np.random.permutation(np.resize(levels, k // 32))).repeat(32)
    a = np.empty((k // 512, 16))
    for p in range(k // 512):
        a[p, :8] = np.random.permutation(np.resize(levels, 8))
        for g in range(8):
            far = levels[np.abs(levels - a[p, g]) >= 10]
            a[p, g + 8] = far[np.random.randint(len(far))]
    return np.exp2(a.ravel()).repeat(32)


def f64(x):
    return np.asarray(x).astype(np.float64)


def striped(idx):
    return np.tile(idx.reshape(-1, 16).T, (8, 1)).astype(np.uint16)


def unstriped(offs):
    return offs[:16].T.reshape(-1).astype(np.int64)


E2M1 = np.array([0.0, 0.5, 1.0, 1.5, 2.0, 3.0, 4.0, 6.0, -0.0, -0.5, -1.0, -1.5, -2.0, -3.0, -4.0, -6.0])


def pack_weight(w, fmt):
    k, n = w.shape
    w = f64(np.asarray(w, np.float32).astype(ml_dtypes.bfloat16)).reshape(k // 32, 32, n)
    amax = np.abs(w).max(1)
    if fmt == "e4m3":
        byte = np.frexp(amax)[1] - 1 + 127 - 7
    else:
        mant, ex = np.frexp(amax / 6.0)
        byte = np.where(mant > 0.5, ex, ex - 1) + 127
    byte = np.clip(np.where(amax > 0, byte, 1), 1, 254)
    scaled = (w * np.exp2(127.0 - byte)[:, None, :]).reshape(k, n).astype(np.float32)
    by_word = np.ascontiguousarray(scaled.reshape(k // 512, 128, 4, n).transpose(0, 1, 3, 2))
    if fmt == "e4m3":
        words = by_word.astype(ml_dtypes.float8_e4m3fn).view(np.uint8)
    else:
        c = by_word.astype(ml_dtypes.float4_e2m1fn).view(np.uint8) & 0xF
        words = (c[..., 0::2] | (c[..., 1::2] << 4)).reshape(k // 512, 128, 2 * n)
    return np.ascontiguousarray(words), np.ascontiguousarray(byte.astype(np.uint8).reshape(k // 512, 16, n))


def unpack_weight(words, scales, fmt):
    g, _, n = scales.shape
    words = np.ascontiguousarray(words).reshape(g, 128, n, -1)
    if fmt == "e4m3":
        vals = words.view(ml_dtypes.float8_e4m3fn).astype(np.float64)
    else:
        nib = np.empty((g, 128, n, 4), np.uint8)
        nib[..., 0::2] = words & 0xF
        nib[..., 1::2] = words >> 4
        vals = E2M1[nib]
    vals = vals * np.repeat(np.exp2(scales.astype(np.float64) - 127.0), 8, axis=1)[..., None]
    return vals.transpose(0, 1, 3, 2).reshape(g * 512, n)


def gelu(v):
    return 0.5 * v * (1.0 + np.tanh(np.sqrt(2.0 / np.pi) * (v + 0.044715 * v**3)))


K, H, T, S, T2, P = 1024, 512, 2048, 1024, 2048, 1024

def setup_inputs():
    n = np.random.standard_normal
    f32 = np.float32
    s = mx_kscale(K)[:, None]
    u = mx_kscale(H)[:, None]
    tab_words, tab_scales = pack_weight(n((K, T)) * s, "e4m3")
    wa_words, wa_scales = pack_weight(n((H, H)) / u * u.T / np.sqrt(2 * H), "e2m1")
    wd_words, wd_scales = pack_weight(n((H, H)) / u * u.T / np.sqrt(2 * H), "e4m3")
    return {
        "tab_words": tab_words, "tab_scales": tab_scales,
        "offs": striped(np.random.permutation(T)[:S]),
        "w1": (n((K, H)) / s * u.T / np.sqrt(K)).astype(f32),
        "page0": (n((H, T2)) * u).astype(f32),
        "offs2": striped(np.random.permutation(T2)[:S]),
        "wgs": np.exp(0.3 * n((128, S))).astype(f32),
        "offs3": striped(np.random.permutation(T2)[:P]),
        "gm": n((H, P)).astype(f32),
        "shift": (0.8 * n(H) * u[:, 0]).astype(f32),
        "wa_words": wa_words, "wa_scales": wa_scales,
        "wb": (n((H, H)) / u * u.T / np.sqrt(2 * H)).astype(f32),
        "wc": (n((H, H)) / u * u.T / np.sqrt(2 * H)).astype(f32),
        "wd_words": wd_words, "wd_scales": wd_scales,
        "cap": ((0.8 + 0.6 * n((H, P))) * u).astype(f32),
        "offs4": striped(np.random.permutation(T2)[:P]),
        "wgo": np.exp(0.3 * n((128, P))).astype(f32),
    }

def reference(tab_words, tab_scales, offs, w1, page0, offs2, wgs, offs3, gm, shift, wa_words, wa_scales, wb, wc, wd_words, wd_scales, cap, offs4, wgo):
    v = unpack_weight(tab_words, tab_scales, "e4m3")[:, unstriped(offs)]
    h = mxq(f64(w1), 0, "e4m3").T @ v
    page = f64(page0).copy()
    page[:, unstriped(offs2)] = np.tile(f64(wgs), (H // 128, 1)) * h
    x = page[:, unstriped(offs3)]
    xg = x * f64(gm)
    xs = x + f64(shift)[:, None]
    xm = np.abs(xs)
    wa = unpack_weight(wa_words, wa_scales, "e2m1")
    wd = unpack_weight(wd_words, wd_scales, "e4m3")
    ya = wa.T @ mxq(x, 0, "e4m3") + mxq(f64(wb), 0, "e4m3").T @ mxq(xg, 0, "e4m3")
    yb = mxq(f64(wc), 0, "e4m3").T @ mxq(xs, 0, "e4m3") + wd.T @ mxq(xm, 0, "e4m3")
    y = np.minimum(np.maximum(ya, yb), f64(cap))
    page[:, unstriped(offs4)] = np.tile(f64(wgo), (H // 128, 1)) * y
    return page

@@ -1,0 +1,285 @@
+from contextlib import ExitStack
+
+import concourse.mybir as mybir
+
+K, H, T, S, T2, J = 1024, 512, 2048, 1024, 2048, 1024
+FLOPS = 2 * K * H * S + 4 * 2 * H * H * J
+
+F32 = mybir.dt.float32
+BF16 = mybir.dt.bfloat16
+I32 = mybir.dt.int32
+U32 = mybir.dt.uint32
+U16 = mybir.dt.uint16
+U8 = mybir.dt.uint8
+FP8X4 = mybir.dt.float8_e4m3fn_x4
+FP4X4 = mybir.dt.float4_e2m1fn_x4
+ALU = mybir.AluOpType
+ACT = mybir.ActivationFunctionType
+
+P = 128
+PACK = 4
+QUAD = 32
+BANK = 512
+CHUNK = 256
+STRIPE = 16
+
+
+def tile_list_door_drive_sheet_kernel(
+    tc, tab_words, tab_scales, offs, w1, page0, offs2, wgs, offs3, gm, shift,
+    wa_words, wa_scales, wb, wc, wd_words, wd_scales, cap, offs4, wgo, out,
+):
+    nc = tc.nc
+    with ExitStack() as ctx:
+        sb = ctx.enter_context(tc.tile_pool(name="sb", bufs=1))
+        ps = ctx.enter_context(tc.psum_pool(name="ps", bufs=1))
+
+        def tile(shape, dtype, name, tag=None, bufs=1):
+            return sb.tile(shape, dtype, name=name, tag=tag or name, bufs=bufs, align_bytes=64)
+
+        def load_list(dram, name):
+            lst = sb.tile([P, dram.shape[1]], U16, name=name)
+            nc.sync.dma_start(lst[:], dram)
+            return lst
+
+        def entries(lst, first, count):
+            return lst[:, first // STRIPE : (first + count) // STRIPE]
+
+        def load_dealt(dst, factors, slots, cols):
+            dealt = factors.rearrange("(q t) j -> q t j", t=PACK)
+            for quad in (0, 2, 1, 3):
+                nc.sync.dma_start(dst[QUAD * quad : QUAD * (quad + 1)], dealt[:, slots, cols])
+
+        def load_weight(rows, name, tag):
+            raw = tile([P, PACK, H], F32, name, tag)
+            nc.sync.dma_start(raw[:], rows.rearrange("(p i) c -> p i c", i=PACK))
+            return raw
+
+        def round_weight(copy, raw, name, tag):
+            woven = tile([P, H * PACK], BF16, name, tag)
+            copy(
+                woven[:].rearrange("p (t m i) -> p m t i", t=PACK, i=PACK),
+                raw[:].rearrange("p i (m t) -> p m t i", t=PACK),
+            )
+            return woven
+
+        def quantize(woven, name):
+            width = woven.shape[1] // PACK
+            codes = tile([P, width], U32, name + "_codes")
+            scales = tile([P, width], U8, name + "_scales")
+            nc.vector.quantize_mx(out=codes[:].bitcast(FP8X4), scales=scales[:], in_=woven[:])
+            return codes, scales
+
+        page_rows = page0.rearrange("(p t) c -> t p c", t=PACK)
+        out_rows = out.rearrange("(p t) c -> t p c", t=PACK)
+
+        list1 = load_list(offs, "list1")
+        tab = [tile([P, T], U32, "tab%d" % a) for a in range(2)]
+        tab_dram = [tab_words[a].rearrange("p n i -> p (n i)").bitcast(I32) for a in range(2)]
+        nc.sync.dma_start(tab[0][:].bitcast(I32), tab_dram[0])
+
+        tab_sc = tile([P, T], U8, "tab_sc")
+        nc.vector.memset(tab_sc[:].bitcast(I32), 0)
+        for quad in range(4):
+            nc.sync.dma_start(
+                tab_sc[QUAD * quad : QUAD * quad + 8, :].bitcast(I32),
+                tab_scales[:, 4 * quad : 4 * quad + 4, :].bitcast(I32),
+            )
+        w_sc_raw = tile([P, H], U8, "w_sc_raw")
+        nc.gpsimd.memset(w_sc_raw[:].bitcast(I32), 0)
+
+        w1_raw = [load_weight(w1[512 * a : 512 * (a + 1), :], "w1_raw%d" % a, "stage%d" % a) for a in range(2)]
+        nc.sync.dma_start(tab[1][:].bitcast(I32), tab_dram[1])
+        list2 = load_list(offs2, "list2")
+
+        page = [tile([P, T2], F32, "page%d" % t) for t in range(PACK)]
+        wgs_sb = tile([P, PACK, S], F32, "wgs_sb", "wgs_then_x")
+        nc.sync.dma_start(page[0][:], page_rows[0])
+        for half in range(2):
+            cols = slice(BANK * half, BANK * (half + 1))
+            load_dealt(wgs_sb[:, 0, cols], wgs, 0, cols)
+        nc.sync.dma_start(page[1][:], page_rows[1])
+        load_dealt(wgs_sb[:, 1, :], wgs, 1, slice(0, S))
+        nc.sync.dma_start(page[2][:], page_rows[2])
+        load_dealt(wgs_sb[:, 2:4, :], wgs, slice(2, 4), slice(0, S))
+        nc.sync.dma_start(page[3][:], page_rows[3])
+
+        v = [tile([P, S], U32, "v%d" % a) for a in range(2)]
+        v_sc = tile([P, S], U8, "v_sc")
+        nc.vector.tensor_copy(v[0][:], tab[0][:].indirect(list1[:]))
+        nc.vector.tensor_copy(v_sc[:], tab_sc[:].indirect(list1[:]))
+        w1_woven = [
+            round_weight(nc.scalar.copy, w1_raw[0], "w1_woven0", "woven0"),
+            round_weight(nc.vector.tensor_copy, w1_raw[1], "w1_woven1", "woven1"),
+        ]
+        w1_q = [quantize(w1_woven[a], "w1_%d" % a) for a in range(2)]
+        for half in range(2):
+            cols = slice(BANK * half, BANK * (half + 1))
+            nc.vector.tensor_copy(v[1][:, cols], tab[1][:].indirect(entries(list1, BANK * half, BANK)))
+
+        for t in range(PACK):
+            rows = slice(P * t, P * (t + 1))
+            h = tile([P, S], F32, "h%d" % t, "h_then_xs", bufs=2)
+            for half in range(2):
+                cols = slice(BANK * half, BANK * (half + 1))
+                h_ps = ps.tile([P, BANK], F32, name="h_ps", tag="h_ps", bufs=2)
+                for a in range(2):
+                    nc.tensor.matmul_mx(
+                        out=h_ps[:],
+                        lhsT=w1_q[a][0][:, rows].bitcast(FP8X4), lhsT_scale=w1_q[a][1][:, rows],
+                        rhs=v[a][:, cols].bitcast(FP8X4), rhs_scale=v_sc[4 * a : P, cols],
+                        start=(a == 0), stop=(a == 1),
+                    )
+                nc.scalar.copy(h[:, cols], h_ps[:])
+                if t == 0:
+                    nc.vector.tensor_tensor(
+                        page[t][:].indirect(entries(list2, BANK * half, BANK)), h[:, cols], wgs_sb[:, t, cols], ALU.mult
+                    )
+            if t > 0:
+                nc.vector.tensor_tensor(page[t][:].indirect(list2[:]), h[:], wgs_sb[:, t, :], ALU.mult)
+
+        wb_raw = load_weight(wb, "wb_raw", "stage0")
+        wc_raw = load_weight(wc, "wc_raw", "stage1")
+        wa_raw = tile([P, 2 * H], U8, "wa_raw")
+        nc.sync.dma_start(wa_raw[:].bitcast(I32), wa_words[0].bitcast(I32))
+        wd_raw = tile([P, H], I32, "wd_raw")
+        nc.sync.dma_start(wd_raw[:], wd_words[0].rearrange("p n i -> p (n i)").bitcast(I32))
+        for first, scales in ((0, wa_scales), (4, wd_scales)):
+            for quad in range(4):
+                nc.sync.dma_start(
+                    w_sc_raw[QUAD * quad + first : QUAD * quad + first + 4, :].bitcast(I32),
+                    scales[0, 4 * quad : 4 * quad + 4, :].bitcast(I32),
+                )
+        list3 = load_list(offs3, "list3")
+        list4 = load_list(offs4, "list4")
+        shift_sb = tile([P, PACK], F32, "shift_sb")
+        nc.sync.dma_start(shift_sb[:], shift.rearrange("(p t) -> p t", t=PACK))
+        gm_sb = tile([P, PACK, J], F32, "gm_sb")
+        nc.sync.dma_start(gm_sb[:], gm.rearrange("(p t) j -> p t j", t=PACK))
+        cap_sb, wgo_sb = [], []
+        for half in range(2):
+            cols = slice(BANK * half, BANK * (half + 1))
+            cap_sb.append(tile([P, PACK, BANK], F32, "cap%d" % half))
+            nc.sync.dma_start(cap_sb[half][:], cap.rearrange("(p t) j -> p t j", t=PACK)[:, :, cols])
+            wgo_sb.append(tile([P, PACK, BANK], F32, "wgo%d" % half))
+            load_dealt(wgo_sb[half][:], wgo, slice(0, PACK), cols)
+
+        wb_q = quantize(round_weight(nc.scalar.copy, wb_raw, "wb_woven", "woven0"), "wb")
+        wc_q = quantize(round_weight(nc.scalar.copy, wc_raw, "wc_woven", "woven1"), "wc")
+        wa_sb = tile([P, 2 * H], U8, "wa_sb")
+        nc.vector.tensor_copy(
+            wa_sb[:].bitcast(U16).rearrange("p (t m) -> p t m", t=PACK),
+            wa_raw[:].bitcast(U16).rearrange("p (m t) -> p t m", t=PACK),
+        )
+        wd_sb = tile([P, H], I32, "wd_sb")
+        nc.vector.tensor_copy(
+            wd_sb[:].rearrange("p (t m) -> p m t", t=PACK), wd_raw[:].rearrange("p (m t) -> p m t", t=PACK)
+        )
+        w_sc = tile([P, H], U8, "w_sc")
+        nc.vector.tensor_copy(
+            w_sc[:].rearrange("p (t m) -> p t m", t=PACK), w_sc_raw[:].rearrange("p (m t) -> p t m", t=PACK)
+        )
+
+        x_all = tile([P, PACK * J], F32, "x_all", "wgs_then_x")
+        spans = ((0, CHUNK), (CHUNK, CHUNK), (2 * CHUNK, 2 * CHUNK))
+        x = [x_all[:, PACK * first : PACK * (first + n)].rearrange("p (t j) -> p t j", t=PACK) for first, n in spans]
+        xs_tiles = [tile([P, PACK * BANK], BF16, "xs%d" % half, "h_then_xs", bufs=2) for half in range(2)]
+        xs = [
+            xs_tiles[0][:, : PACK * CHUNK].rearrange("p (t j) -> p t j", t=PACK),
+            xs_tiles[0][:, PACK * CHUNK :].rearrange("p (t j) -> p t j", t=PACK),
+            xs_tiles[1][:].rearrange("p (t j) -> p t j", t=PACK),
+        ]
+        xg = {}
+
+        def pick(span):
+            first, n = spans[span]
+            for t in range(PACK):
+                nc.vector.tensor_copy(x[span][:, t, :], page[t][:].indirect(entries(list3, first, n)))
+                nc.scalar.activation(xs[span][:, t, :], x[span][:, t, :], ACT.Identity, bias=shift_sb[:, t : t + 1])
+
+        def gate(span, tag):
+            first, n = spans[span]
+            xg[span] = tile([P, PACK, n], BF16, "xg%d" % span, tag)
+            nc.vector.tensor_tensor(xg[span][:], x[span], gm_sb[:, :, first : first + n], ALU.mult)
+
+        woven_tags = ("woven_first", "stage0", "stage1", "woven_last")
+        woven, act_q = {}, {}
+
+        def weave(chunk, which):
+            span = min(chunk, 2)
+            cols = slice(CHUNK * (chunk - span), CHUNK * (chunk - span + 1))
+            if chunk not in woven:
+                woven[chunk] = tile([P, 4 * PACK * CHUNK], BF16, "woven_act%d" % chunk, woven_tags[chunk])
+            part = lambda o: woven[chunk][:, o * PACK * CHUNK : (o + 1) * PACK * CHUNK]
+            for o in which:
+                if o == 3:
+                    nc.scalar.activation(part(3), part(2), ACT.Abs)
+                else:
+                    nc.scalar.copy(
+                        part(o).rearrange("p (c i t) -> p c t i", i=4, t=PACK),
+                        (x, xg, xs)[o][span][:, :, cols].rearrange("p t (c i) -> p c t i", i=4),
+                    )
+
+        def judge(pieces, tag):
+            ya_ps = ps.tile([P, 2, CHUNK], F32, name="ya_ps", tag="ya_ps", bufs=3)
+            yb_ps = ps.tile([P, 2, CHUNK], F32, name="yb_ps", tag="yb_ps", bufs=3)
+            for n, (t, chunk) in enumerate(pieces):
+                rows = slice(P * t, P * (t + 1))
+                weights = (
+                    (wa_sb[:, 2 * P * t : 2 * P * (t + 1)].bitcast(FP4X4), w_sc[:, rows]),
+                    (wb_q[0][:, rows].bitcast(FP8X4), wb_q[1][:, rows]),
+                    (wc_q[0][:, rows].bitcast(FP8X4), wc_q[1][:, rows]),
+                    (wd_sb[:, rows].bitcast(FP8X4), w_sc[4:P, rows]),
+                )
+                codes, scales = act_q[chunk]
+                for o in range(4):
+                    cols = slice(CHUNK * o, CHUNK * (o + 1))
+                    nc.tensor.matmul_mx(
+                        out=(ya_ps if o < 2 else yb_ps)[:, n, :],
+                        lhsT=weights[o][0], lhsT_scale=weights[o][1],
+                        rhs=codes[:, cols].bitcast(FP8X4), rhs_scale=scales[:, cols],
+                        start=(o % 2 == 0), stop=(o % 2 == 1),
+                    )
+            ya = tile([P, 2, CHUNK], F32, "ya", bufs=3)
+            nc.scalar.copy(ya[:], ya_ps[:])
+            y = tile([P, 2, CHUNK], F32, "y", tag, bufs=3 if tag == "y" else 1)
+            nc.vector.tensor_tensor(y[:], ya[:], yb_ps[:], ALU.max)
+            (t0, c0), (t1, c1) = pieces
+            half = c0 // 2
+            if t0 == t1:
+                nc.vector.tensor_tensor(
+                    y[:], y[:], cap_sb[half][:, t0, :].rearrange("p (n j) -> p n j", n=2), ALU.min
+                )
+                nc.vector.tensor_tensor(
+                    page[t0][:].indirect(entries(list4, CHUNK * c0, 2 * CHUNK)),
+                    y[:].rearrange("p n j -> p (n j)"), wgo_sb[half][:, t0, :], ALU.mult,
+                )
+            else:
+                cols = slice(CHUNK * (c0 % 2), CHUNK * (c0 % 2 + 1))
+                nc.vector.tensor_tensor(y[:], y[:], cap_sb[half][:, t0 : t1 + 1, cols], ALU.min)
+                for n, (t, chunk) in enumerate(pieces):
+                    nc.vector.tensor_tensor(
+                        page[t][:].indirect(entries(list4, CHUNK * chunk, CHUNK)),
+                        y[:, n, :], wgo_sb[half][:, t, cols], ALU.mult,
+                    )
+
+        pick(0)
+        gate(0, "xg0")
+        weave(0, (0, 2, 3, 1))
+        pick(1)
+        gate(1, "xg1")
+        pick(2)
+        act_q[0] = quantize(woven[0], "act0")
+        gate(2, "woven_first")
+        weave(1, (0, 2, 3, 1))
+        judge([(0, 0), (1, 0)], "y")
+        act_q[1] = quantize(woven[1], "act1")
+        judge([(2, 0), (3, 0)], "stage0")
+        weave(2, (0, 2, 3, 1))
+        act_q[2] = quantize(woven[2], "act2")
+        judge([(0, 1), (1, 1)], "stage1")
+        weave(3, (0, 2, 3, 1))
+        act_q[3] = quantize(woven[3], "act3")
+        judge([(2, 1), (3, 1)], "woven_last")
+        for t in range(PACK):
+            judge([(t, 2), (t, 3)], "y")
+            nc.sync.dma_start(out_rows[t], page[t][:])

@@ -54,19 +54,17 @@ def tile_list_door_drive_sheet_kernel(
             nc.sync.dma_start(raw[:], rows.rearrange("(p i) c -> p i c", i=PACK))
             return raw
 
-        def round_weight(copy, raw, name, tag):
-            woven = tile([P, H * PACK], BF16, name, tag)
+        def round_weight(copy, raw, woven):
             copy(
-                woven[:].rearrange("p (t m i) -> p m t i", t=PACK, i=PACK),
+                woven.rearrange("p (t m i) -> p m t i", t=PACK, i=PACK),
                 raw[:].rearrange("p i (m t) -> p m t i", t=PACK),
             )
-            return woven
 
-        def quantize(woven, name):
+        def quantize(woven, name, tag=None):
             width = woven.shape[1] // PACK
-            codes = tile([P, width], U32, name + "_codes")
+            codes = tile([P, width], U32, name + "_codes", tag)
             scales = tile([P, width], U8, name + "_scales")
-            nc.vector.quantize_mx(out=codes[:].bitcast(FP8X4), scales=scales[:], in_=woven[:])
+            nc.vector.quantize_mx(out=codes[:].bitcast(FP8X4), scales=scales[:], in_=woven)
             return codes, scales
 
         page_rows = page0.rearrange("(p t) c -> t p c", t=PACK)
@@ -100,25 +98,30 @@ def tile_list_door_drive_sheet_kernel(
         nc.sync.dma_start(page[1][:], page_rows[1])
         load_dealt(wgs_sb[:, 1, :], wgs, 1, slice(0, S))
         nc.sync.dma_start(page[2][:], page_rows[2])
-        load_dealt(wgs_sb[:, 2:4, :], wgs, slice(2, 4), slice(0, S))
-        nc.sync.dma_start(page[3][:], page_rows[3])
+        load_dealt(wgs_sb[:, 2, :], wgs, 2, slice(0, S))
 
         v = [tile([P, S], U32, "v%d" % a) for a in range(2)]
         v_sc = tile([P, S], U8, "v_sc")
         nc.vector.tensor_copy(v[0][:], tab[0][:].indirect(list1[:]))
         nc.vector.tensor_copy(v_sc[:], tab_sc[:].indirect(list1[:]))
-        w1_woven = [
-            round_weight(nc.scalar.copy, w1_raw[0], "w1_woven0", "woven0"),
-            round_weight(nc.vector.tensor_copy, w1_raw[1], "w1_woven1", "woven1"),
-        ]
-        w1_q = [quantize(w1_woven[a], "w1_%d" % a) for a in range(2)]
+        w1_woven = tile([P, 2, PACK * H], BF16, "w1_woven", "woven_weights")
+        round_weight(nc.scalar.copy, w1_raw[0], w1_woven[:, 0, :])
+        round_weight(nc.vector.tensor_copy, w1_raw[1], w1_woven[:, 1, :])
+        w1_q = [quantize(w1_woven[:, a, :], "w1_%d" % a) for a in range(2)]
+        wb_raw = load_weight(wb, "wb_raw", "stage0")
+        list3 = load_list(offs3, "list3")
+        shift_sb = tile([P, PACK], F32, "shift_sb")
+        nc.sync.dma_start(shift_sb[:], shift.rearrange("(p t) -> p t", t=PACK))
+        nc.sync.dma_start(page[3][:], page_rows[3])
+        load_dealt(wgs_sb[:, 3, :], wgs, 3, slice(0, S))
+        wc_raw = load_weight(wc, "wc_raw", "stage1")
         for half in range(2):
             cols = slice(BANK * half, BANK * (half + 1))
             nc.vector.tensor_copy(v[1][:, cols], tab[1][:].indirect(entries(list1, BANK * half, BANK)))
 
         for t in range(PACK):
             rows = slice(P * t, P * (t + 1))
-            h = tile([P, S], F32, "h%d" % t, "h_then_xs", bufs=2)
+            h = tile([P, S], F32, "h%d" % t, ("h_even", "h_odd")[t % 2])
             for half in range(2):
                 cols = slice(BANK * half, BANK * (half + 1))
                 h_ps = ps.tile([P, BANK], F32, name="h_ps", tag="h_ps", bufs=2)
@@ -137,8 +140,8 @@ def tile_list_door_drive_sheet_kernel(
             if t > 0:
                 nc.vector.tensor_tensor(page[t][:].indirect(list2[:]), h[:], wgs_sb[:, t, :], ALU.mult)
 
-        wb_raw = load_weight(wb, "wb_raw", "stage0")
-        wc_raw = load_weight(wc, "wc_raw", "stage1")
+        gm_sb = tile([P, PACK, J], F32, "gm_sb")
+        nc.sync.dma_start(gm_sb[:], gm.rearrange("(p t) j -> p t j", t=PACK))
         wa_raw = tile([P, 2 * H], U8, "wa_raw")
         nc.sync.dma_start(wa_raw[:].bitcast(I32), wa_words[0].bitcast(I32))
         wd_raw = tile([P, H], I32, "wd_raw")
@@ -149,12 +152,7 @@ def tile_list_door_drive_sheet_kernel(
                     w_sc_raw[QUAD * quad + first : QUAD * quad + first + 4, :].bitcast(I32),
                     scales[0, 4 * quad : 4 * quad + 4, :].bitcast(I32),
                 )
-        list3 = load_list(offs3, "list3")
         list4 = load_list(offs4, "list4")
-        shift_sb = tile([P, PACK], F32, "shift_sb")
-        nc.sync.dma_start(shift_sb[:], shift.rearrange("(p t) -> p t", t=PACK))
-        gm_sb = tile([P, PACK, J], F32, "gm_sb")
-        nc.sync.dma_start(gm_sb[:], gm.rearrange("(p t) j -> p t j", t=PACK))
         cap_sb, wgo_sb = [], []
         for half in range(2):
             cols = slice(BANK * half, BANK * (half + 1))
@@ -163,26 +161,13 @@ def tile_list_door_drive_sheet_kernel(
             wgo_sb.append(tile([P, PACK, BANK], F32, "wgo%d" % half))
             load_dealt(wgo_sb[half][:], wgo, slice(0, PACK), cols)
 
-        wb_q = quantize(round_weight(nc.scalar.copy, wb_raw, "wb_woven", "woven0"), "wb")
-        wc_q = quantize(round_weight(nc.scalar.copy, wc_raw, "wc_woven", "woven1"), "wc")
-        wa_sb = tile([P, 2 * H], U8, "wa_sb")
-        nc.vector.tensor_copy(
-            wa_sb[:].bitcast(U16).rearrange("p (t m) -> p t m", t=PACK),
-            wa_raw[:].bitcast(U16).rearrange("p (m t) -> p t m", t=PACK),
-        )
-        wd_sb = tile([P, H], I32, "wd_sb")
-        nc.vector.tensor_copy(
-            wd_sb[:].rearrange("p (t m) -> p m t", t=PACK), wd_raw[:].rearrange("p (m t) -> p m t", t=PACK)
-        )
-        w_sc = tile([P, H], U8, "w_sc")
-        nc.vector.tensor_copy(
-            w_sc[:].rearrange("p (t m) -> p t m", t=PACK), w_sc_raw[:].rearrange("p (m t) -> p t m", t=PACK)
-        )
-
+        wbc_woven = tile([P, 2, PACK * H], BF16, "wbc_woven", "woven_weights")
+        round_weight(nc.scalar.copy, wb_raw, wbc_woven[:, 0, :])
+        round_weight(nc.scalar.copy, wc_raw, wbc_woven[:, 1, :])
         x_all = tile([P, PACK * J], F32, "x_all", "wgs_then_x")
         spans = ((0, CHUNK), (CHUNK, CHUNK), (2 * CHUNK, 2 * CHUNK))
         x = [x_all[:, PACK * first : PACK * (first + n)].rearrange("p (t j) -> p t j", t=PACK) for first, n in spans]
-        xs_tiles = [tile([P, PACK * BANK], BF16, "xs%d" % half, "h_then_xs", bufs=2) for half in range(2)]
+        xs_tiles = [tile([P, PACK * BANK], BF16, "xs%d" % half, ("stage1", "h_even")[half]) for half in range(2)]
         xs = [
             xs_tiles[0][:, : PACK * CHUNK].rearrange("p (t j) -> p t j", t=PACK),
             xs_tiles[0][:, PACK * CHUNK :].rearrange("p (t j) -> p t j", t=PACK),
@@ -219,15 +204,16 @@ def tile_list_door_drive_sheet_kernel(
                         (x, xg, xs)[o][span][:, :, cols].rearrange("p t (c i) -> p c t i", i=4),
                     )
 
-        def judge(pieces, tag):
+        def products(pair, chunk):
             ya_ps = ps.tile([P, 2, CHUNK], F32, name="ya_ps", tag="ya_ps", bufs=3)
             yb_ps = ps.tile([P, 2, CHUNK], F32, name="yb_ps", tag="yb_ps", bufs=3)
-            for n, (t, chunk) in enumerate(pieces):
+            for n, t in enumerate((2 * pair, 2 * pair + 1)):
                 rows = slice(P * t, P * (t + 1))
+                rows_c = slice(H + P * t, H + P * (t + 1))
                 weights = (
                     (wa_sb[:, 2 * P * t : 2 * P * (t + 1)].bitcast(FP4X4), w_sc[:, rows]),
-                    (wb_q[0][:, rows].bitcast(FP8X4), wb_q[1][:, rows]),
-                    (wc_q[0][:, rows].bitcast(FP8X4), wc_q[1][:, rows]),
+                    (wbc_codes[:, rows].bitcast(FP8X4), wbc_scales[:, rows]),
+                    (wbc_codes[:, rows_c].bitcast(FP8X4), wbc_scales[:, rows_c]),
                     (wd_sb[:, rows].bitcast(FP8X4), w_sc[4:P, rows]),
                 )
                 codes, scales = act_q[chunk]
@@ -241,45 +227,83 @@ def tile_list_door_drive_sheet_kernel(
                     )
             ya = tile([P, 2, CHUNK], F32, "ya", bufs=3)
             nc.scalar.copy(ya[:], ya_ps[:])
-            y = tile([P, 2, CHUNK], F32, "y", tag, bufs=3 if tag == "y" else 1)
-            nc.vector.tensor_tensor(y[:], ya[:], yb_ps[:], ALU.max)
-            (t0, c0), (t1, c1) = pieces
-            half = c0 // 2
-            if t0 == t1:
-                nc.vector.tensor_tensor(
-                    y[:], y[:], cap_sb[half][:, t0, :].rearrange("p (n j) -> p n j", n=2), ALU.min
-                )
-                nc.vector.tensor_tensor(
-                    page[t0][:].indirect(entries(list4, CHUNK * c0, 2 * CHUNK)),
-                    y[:].rearrange("p n j -> p (n j)"), wgo_sb[half][:, t0, :], ALU.mult,
-                )
-            else:
-                cols = slice(CHUNK * (c0 % 2), CHUNK * (c0 % 2 + 1))
-                nc.vector.tensor_tensor(y[:], y[:], cap_sb[half][:, t0 : t1 + 1, cols], ALU.min)
-                for n, (t, chunk) in enumerate(pieces):
-                    nc.vector.tensor_tensor(
-                        page[t][:].indirect(entries(list4, CHUNK * chunk, CHUNK)),
-                        y[:, n, :], wgo_sb[half][:, t, cols], ALU.mult,
-                    )
+            return ya, yb_ps
+
+        def columns(chunk):
+            return slice(CHUNK * (chunk % 2), CHUNK * (chunk % 2 + 1))
+
+        def larger(y, pair, chunk):
+            ya, yb_ps = products(pair, chunk)
+            nc.vector.tensor_tensor(y[:, 2 * pair : 2 * pair + 2, columns(chunk)], ya[:], yb_ps[:], ALU.max)
+
+        def limit(y, pair, chunk):
+            part = y[:, 2 * pair : 2 * pair + 2, columns(chunk)]
+            nc.vector.tensor_tensor(part, part, cap_sb[chunk // 2][:, 2 * pair : 2 * pair + 2, columns(chunk)], ALU.min)
+
+        def rewrite(y, t, chunk, count=1):
+            cols = slice(columns(chunk).start, columns(chunk).start + count * CHUNK)
+            nc.vector.tensor_tensor(
+                page[t][:].indirect(entries(list4, CHUNK * chunk, CHUNK * count)),
+                y[:, t, cols], wgo_sb[chunk // 2][:, t, cols], ALU.mult,
+            )
+
+        def store(t):
+            nc.sync.dma_start(out_rows[t], page[t][:])
 
         pick(0)
         gate(0, "xg0")
         weave(0, (0, 2, 3, 1))
         pick(1)
         gate(1, "xg1")
-        pick(2)
-        act_q[0] = quantize(woven[0], "act0")
-        gate(2, "woven_first")
         weave(1, (0, 2, 3, 1))
-        judge([(0, 0), (1, 0)], "y")
-        act_q[1] = quantize(woven[1], "act1")
-        judge([(2, 0), (3, 0)], "stage0")
-        weave(2, (0, 2, 3, 1))
-        act_q[2] = quantize(woven[2], "act2")
-        judge([(0, 1), (1, 1)], "stage1")
+        pick(2)
+        wbc_codes, wbc_scales = quantize(wbc_woven[:].rearrange("p a c -> p (a c)"), "wbc", "h_odd")
+        wa_sb = tile([P, 2 * H], U8, "wa_sb")
+        nc.vector.tensor_copy(
+            wa_sb[:].bitcast(U16).rearrange("p (t m) -> p t m", t=PACK),
+            wa_raw[:].bitcast(U16).rearrange("p (m t) -> p t m", t=PACK),
+        )
+        wd_sb = tile([P, H], I32, "wd_sb")
+        nc.vector.tensor_copy(
+            wd_sb[:].rearrange("p (t m) -> p m t", t=PACK), wd_raw[:].rearrange("p (m t) -> p m t", t=PACK)
+        )
+        w_sc = tile([P, H], U8, "w_sc")
+        nc.vector.tensor_copy(
+            w_sc[:].rearrange("p (t m) -> p t m", t=PACK), w_sc_raw[:].rearrange("p (m t) -> p t m", t=PACK)
+        )
+
+        act_q[0] = quantize(woven[0][:], "act0")
+        gate(2, "woven_first")
+        for chunk in range(2):
+            if chunk == 1:
+                weave(2, (0, 2, 3, 1))
+            act_q[chunk + 1] = quantize(woven[chunk + 1][:], "act%d" % (chunk + 1), (None, "stage0")[chunk])
+            y = tile([P, PACK, BANK], F32, "y%d" % chunk, woven_tags[chunk + 1])
+            for pair in range(2):
+                larger(y, pair, chunk)
+            for pair in range(2):
+                limit(y, pair, chunk)
+            for t in range(PACK):
+                rewrite(y, t, chunk)
         weave(3, (0, 2, 3, 1))
-        act_q[3] = quantize(woven[3], "act3")
-        judge([(2, 1), (3, 1)], "woven_last")
-        for t in range(PACK):
-            judge([(t, 2), (t, 3)], "y")
-            nc.sync.dma_start(out_rows[t], page[t][:])
+        act_q[3] = quantize(woven[3][:], "act3", "stage1")
+        y = tile([P, PACK, BANK], F32, "y2", woven_tags[3])
+        for pair in range(2):
+            larger(y, pair, 2)
+        for pair in range(2):
+            limit(y, pair, 2)
+        rewrite(y, 0, 2)
+        rewrite(y, 1, 2)
+        larger(y, 0, 3)
+        rewrite(y, 2, 2)
+        limit(y, 0, 3)
+        larger(y, 1, 3)
+        rewrite(y, 0, 3)
+        store(0)
+        limit(y, 1, 3)
+        rewrite(y, 1, 3)
+        store(1)
+        rewrite(y, 2, 3)
+        store(2)
+        rewrite(y, 3, 2, 2)
+        store(3)

@@ -52,12 +52,12 @@ def tile_list_door_drive_sheet_kernel(
         def load_weight(rows, name, tag):
             raw = tile([P, PACK, H], F32, name, tag)
             nc.sync.dma_start(raw[:], rows.rearrange("(p i) c -> p i c", i=PACK))
-            return raw
+            return raw[:]
 
         def round_weight(copy, raw, woven):
             copy(
                 woven.rearrange("p (t m i) -> p m t i", t=PACK, i=PACK),
-                raw[:].rearrange("p i (m t) -> p m t i", t=PACK),
+                raw.rearrange("p i (m t) -> p m t i", t=PACK),
             )
 
         def quantize(woven, name, tag=None):
@@ -90,7 +90,9 @@ def tile_list_door_drive_sheet_kernel(
         list2 = load_list(offs2, "list2")
 
         page = [tile([P, T2], F32, "page%d" % t) for t in range(PACK)]
-        wgs_sb = tile([P, PACK, S], F32, "wgs_sb", "wgs_then_x")
+        wgs_wc = tile([P, PACK * (S + H)], F32, "wgs_wc", "wgs_then_x")
+        wgs_sb = wgs_wc[:, : PACK * S].rearrange("p (t j) -> p t j", t=PACK)
+        wc_raw = wgs_wc[:, PACK * S :].rearrange("p (i c) -> p i c", i=PACK)
         nc.sync.dma_start(page[0][:], page_rows[0])
         for half in range(2):
             cols = slice(BANK * half, BANK * (half + 1))
@@ -108,13 +110,16 @@ def tile_list_door_drive_sheet_kernel(
         round_weight(nc.scalar.copy, w1_raw[0], w1_woven[:, 0, :])
         round_weight(nc.vector.tensor_copy, w1_raw[1], w1_woven[:, 1, :])
         w1_q = [quantize(w1_woven[:, a, :], "w1_%d" % a) for a in range(2)]
-        wb_raw = load_weight(wb, "wb_raw", "stage0")
         list3 = load_list(offs3, "list3")
         shift_sb = tile([P, PACK], F32, "shift_sb")
         nc.sync.dma_start(shift_sb[:], shift.rearrange("(p t) -> p t", t=PACK))
         nc.sync.dma_start(page[3][:], page_rows[3])
         load_dealt(wgs_sb[:, 3, :], wgs, 3, slice(0, S))
-        wc_raw = load_weight(wc, "wc_raw", "stage1")
+        gm_rows = gm.rearrange("(p t) j -> p t j", t=PACK)
+        gm_first = tile([P, PACK, CHUNK], F32, "gm_first")
+        nc.sync.dma_start(gm_first[:], gm_rows[:, :, :CHUNK])
+        wb_raw = load_weight(wb, "wb_raw", "stage0")
+        nc.sync.dma_start(wc_raw, wc.rearrange("(p i) c -> p i c", i=PACK))
         for half in range(2):
             cols = slice(BANK * half, BANK * (half + 1))
             nc.vector.tensor_copy(v[1][:, cols], tab[1][:].indirect(entries(list1, BANK * half, BANK)))
@@ -140,8 +145,8 @@ def tile_list_door_drive_sheet_kernel(
             if t > 0:
                 nc.vector.tensor_tensor(page[t][:].indirect(list2[:]), h[:], wgs_sb[:, t, :], ALU.mult)
 
-        gm_sb = tile([P, PACK, J], F32, "gm_sb")
-        nc.sync.dma_start(gm_sb[:], gm.rearrange("(p t) j -> p t j", t=PACK))
+        gm_rest = tile([P, PACK, J - CHUNK], F32, "gm_rest")
+        nc.sync.dma_start(gm_rest[:], gm_rows[:, :, CHUNK:])
         wa_raw = tile([P, 2 * H], U8, "wa_raw")
         nc.sync.dma_start(wa_raw[:].bitcast(I32), wa_words[0].bitcast(I32))
         wd_raw = tile([P, H], I32, "wd_raw")
@@ -164,45 +169,39 @@ def tile_list_door_drive_sheet_kernel(
         wbc_woven = tile([P, 2, PACK * H], BF16, "wbc_woven", "woven_weights")
         round_weight(nc.scalar.copy, wb_raw, wbc_woven[:, 0, :])
         round_weight(nc.scalar.copy, wc_raw, wbc_woven[:, 1, :])
-        x_all = tile([P, PACK * J], F32, "x_all", "wgs_then_x")
-        spans = ((0, CHUNK), (CHUNK, CHUNK), (2 * CHUNK, 2 * CHUNK))
-        x = [x_all[:, PACK * first : PACK * (first + n)].rearrange("p (t j) -> p t j", t=PACK) for first, n in spans]
-        xs_tiles = [tile([P, PACK * BANK], BF16, "xs%d" % half, ("stage1", "h_even")[half]) for half in range(2)]
-        xs = [
-            xs_tiles[0][:, : PACK * CHUNK].rearrange("p (t j) -> p t j", t=PACK),
-            xs_tiles[0][:, PACK * CHUNK :].rearrange("p (t j) -> p t j", t=PACK),
-            xs_tiles[1][:].rearrange("p (t j) -> p t j", t=PACK),
-        ]
+        x = tile([P, 4, PACK, CHUNK], F32, "x", "wgs_then_x")
         xg = {}
 
-        def pick(span):
-            first, n = spans[span]
+        def pick(chunk):
             for t in range(PACK):
-                nc.vector.tensor_copy(x[span][:, t, :], page[t][:].indirect(entries(list3, first, n)))
-                nc.scalar.activation(xs[span][:, t, :], x[span][:, t, :], ACT.Identity, bias=shift_sb[:, t : t + 1])
+                nc.vector.tensor_copy(x[:, chunk, t, :], page[t][:].indirect(entries(list3, CHUNK * chunk, CHUNK)))
 
-        def gate(span, tag):
-            first, n = spans[span]
-            xg[span] = tile([P, PACK, n], BF16, "xg%d" % span, tag)
-            nc.vector.tensor_tensor(xg[span][:], x[span], gm_sb[:, :, first : first + n], ALU.mult)
+        def gate(chunk, engine, tag):
+            xg[chunk] = tile([P, PACK, CHUNK], BF16, "xg%d" % chunk, tag)
+            factors = gm_rest[:, :, CHUNK * (chunk - 1) : CHUNK * chunk] if chunk else gm_first[:]
+            engine.tensor_tensor(xg[chunk][:], x[:, chunk], factors, ALU.mult)
 
-        woven_tags = ("woven_first", "stage0", "stage1", "woven_last")
-        woven, act_q = {}, {}
+        woven_tags = ("stage1", "stage0", "woven_third", "woven_last")
+        woven, act_q, ya = {}, {}, {}
 
-        def weave(chunk, which):
-            span = min(chunk, 2)
-            cols = slice(CHUNK * (chunk - span), CHUNK * (chunk - span + 1))
-            if chunk not in woven:
-                woven[chunk] = tile([P, 4 * PACK * CHUNK], BF16, "woven_act%d" % chunk, woven_tags[chunk])
-            part = lambda o: woven[chunk][:, o * PACK * CHUNK : (o + 1) * PACK * CHUNK]
-            for o in which:
-                if o == 3:
-                    nc.scalar.activation(part(3), part(2), ACT.Abs)
-                else:
-                    nc.scalar.copy(
-                        part(o).rearrange("p (c i t) -> p c t i", i=4, t=PACK),
-                        (x, xg, xs)[o][span][:, :, cols].rearrange("p t (c i) -> p c t i", i=4),
-                    )
+        def weave(chunk):
+            work = tile([P, 5 * PACK * CHUNK], BF16, "woven_act%d" % chunk, woven_tags[chunk])
+            woven[chunk] = work[:, : 4 * PACK * CHUNK]
+            part = lambda o: work[:, o * PACK * CHUNK : (o + 1) * PACK * CHUNK]
+            xs = part(4).rearrange("p (t j) -> p t j", t=PACK)
+            for t in range(PACK):
+                nc.scalar.activation(xs[:, t, :], x[:, chunk, t, :], ACT.Identity, bias=shift_sb[:, t : t + 1])
+
+            def interleave(o, planes):
+                nc.scalar.copy(
+                    part(o).rearrange("p (c i t) -> p c t i", i=4, t=PACK),
+                    planes.rearrange("p t (c i) -> p c t i", i=4),
+                )
+
+            interleave(0, x[:, chunk])
+            interleave(2, xs)
+            nc.scalar.activation(part(3), part(2), ACT.Abs)
+            interleave(1, xg[chunk][:])
 
         def products(pair, chunk):
             ya_ps = ps.tile([P, 2, CHUNK], F32, name="ya_ps", tag="ya_ps", bufs=3)
@@ -225,16 +224,17 @@ def tile_list_door_drive_sheet_kernel(
                         rhs=codes[:, cols].bitcast(FP8X4), rhs_scale=scales[:, cols],
                         start=(o % 2 == 0), stop=(o % 2 == 1),
                     )
-            ya = tile([P, 2, CHUNK], F32, "ya", bufs=3)
-            nc.scalar.copy(ya[:], ya_ps[:])
-            return ya, yb_ps
+            if pair == 0:
+                ya[chunk] = tile([P, PACK, CHUNK], F32, "ya%d" % chunk, ("xg1", "ya_odd", "ya_even", "ya_odd")[chunk])
+            nc.scalar.copy(ya[chunk][:, 2 * pair : 2 * pair + 2, :], ya_ps[:])
+            return ya[chunk][:, 2 * pair : 2 * pair + 2, :], yb_ps
 
         def columns(chunk):
             return slice(CHUNK * (chunk % 2), CHUNK * (chunk % 2 + 1))
 
         def larger(y, pair, chunk):
-            ya, yb_ps = products(pair, chunk)
-            nc.vector.tensor_tensor(y[:, 2 * pair : 2 * pair + 2, columns(chunk)], ya[:], yb_ps[:], ALU.max)
+            ya_pair, yb_ps = products(pair, chunk)
+            nc.vector.tensor_tensor(y[:, 2 * pair : 2 * pair + 2, columns(chunk)], ya_pair, yb_ps[:], ALU.max)
 
         def limit(y, pair, chunk):
             part = y[:, 2 * pair : 2 * pair + 2, columns(chunk)]
@@ -250,13 +250,12 @@ def tile_list_door_drive_sheet_kernel(
         def store(t):
             nc.sync.dma_start(out_rows[t], page[t][:])
 
-        pick(0)
-        gate(0, "xg0")
-        weave(0, (0, 2, 3, 1))
-        pick(1)
-        gate(1, "xg1")
-        weave(1, (0, 2, 3, 1))
-        pick(2)
+        for chunk in range(4):
+            pick(chunk)
+            if chunk < 3:
+                gate(chunk, nc.gpsimd, None)
+            if chunk < 2:
+                weave(chunk)
         wbc_codes, wbc_scales = quantize(wbc_woven[:].rearrange("p a c -> p (a c)"), "wbc", "h_odd")
         wa_sb = tile([P, 2 * H], U8, "wa_sb")
         nc.vector.tensor_copy(
@@ -272,12 +271,12 @@ def tile_list_door_drive_sheet_kernel(
             w_sc[:].rearrange("p (t m) -> p t m", t=PACK), w_sc_raw[:].rearrange("p (m t) -> p t m", t=PACK)
         )
 
-        act_q[0] = quantize(woven[0][:], "act0")
-        gate(2, "woven_first")
+        act_q[0] = quantize(woven[0], "act0")
+        gate(3, nc.vector, "stage1")
         for chunk in range(2):
             if chunk == 1:
-                weave(2, (0, 2, 3, 1))
-            act_q[chunk + 1] = quantize(woven[chunk + 1][:], "act%d" % (chunk + 1), (None, "stage0")[chunk])
+                weave(2)
+            act_q[chunk + 1] = quantize(woven[chunk + 1], "act%d" % (chunk + 1), (None, "stage0")[chunk])
             y = tile([P, PACK, BANK], F32, "y%d" % chunk, woven_tags[chunk + 1])
             for pair in range(2):
                 larger(y, pair, chunk)
@@ -285,8 +284,8 @@ def tile_list_door_drive_sheet_kernel(
                 limit(y, pair, chunk)
             for t in range(PACK):
                 rewrite(y, t, chunk)
-        weave(3, (0, 2, 3, 1))
-        act_q[3] = quantize(woven[3][:], "act3", "stage1")
+        weave(3)
+        act_q[3] = quantize(woven[3], "act3", "woven_third")
         y = tile([P, PACK, BANK], F32, "y2", woven_tags[3])
         for pair in range(2):
             larger(y, pair, 2)

@@ -18,10 +18,16 @@ ACT = mybir.ActivationFunctionType
 
 P = 128
 PACK = 4
+K_PASS = P * PACK
+PASSES = K // K_PASS
 QUAD = 32
-BANK = 512
-CHUNK = 256
+SCALE_ROWS = 4
 STRIPE = 16
+HALF = 512
+CHUNK = 256
+CHUNKS = J // CHUNK
+OPERANDS = 4
+LINE = 4
 
 
 def tile_list_door_drive_sheet_kernel(
@@ -33,8 +39,8 @@ def tile_list_door_drive_sheet_kernel(
         sb = ctx.enter_context(tc.tile_pool(name="sb", bufs=1))
         ps = ctx.enter_context(tc.psum_pool(name="ps", bufs=1))
 
-        def tile(shape, dtype, name, tag=None, bufs=1):
-            return sb.tile(shape, dtype, name=name, tag=tag or name, bufs=bufs, align_bytes=64)
+        def tile(shape, dtype, name, tag=None):
+            return sb.tile(shape, dtype, name=name, tag=tag or name, bufs=1, align_bytes=64)
 
         def load_list(dram, name):
             lst = sb.tile([P, dram.shape[1]], U16, name=name)
@@ -54,38 +60,40 @@ def tile_list_door_drive_sheet_kernel(
             nc.sync.dma_start(raw[:], rows.rearrange("(p i) c -> p i c", i=PACK))
             return raw[:]
 
-        def round_weight(copy, raw, woven):
+        def round_weight(copy, raw, rounded):
             copy(
-                woven.rearrange("p (t m i) -> p m t i", t=PACK, i=PACK),
+                rounded.rearrange("p (t m i) -> p m t i", t=PACK, i=PACK),
                 raw.rearrange("p i (m t) -> p m t i", t=PACK),
             )
 
-        def quantize(woven, name, tag=None):
-            width = woven.shape[1] // PACK
+        def quantize(values, name, tag=None):
+            width = values.shape[1] // PACK
             codes = tile([P, width], U32, name + "_codes", tag)
             scales = tile([P, width], U8, name + "_scales")
-            nc.vector.quantize_mx(out=codes[:].bitcast(FP8X4), scales=scales[:], in_=woven)
+            nc.vector.quantize_mx(out=codes[:].bitcast(FP8X4), scales=scales[:], in_=values)
             return codes, scales
 
         page_rows = page0.rearrange("(p t) c -> t p c", t=PACK)
         out_rows = out.rearrange("(p t) c -> t p c", t=PACK)
 
         list1 = load_list(offs, "list1")
-        tab = [tile([P, T], U32, "tab%d" % a) for a in range(2)]
-        tab_dram = [tab_words[a].rearrange("p n i -> p (n i)").bitcast(I32) for a in range(2)]
+        tab = [tile([P, T], U32, "tab%d" % a) for a in range(PASSES)]
+        tab_dram = [tab_words[a].rearrange("p n i -> p (n i)").bitcast(I32) for a in range(PASSES)]
         nc.sync.dma_start(tab[0][:].bitcast(I32), tab_dram[0])
 
         tab_sc = tile([P, T], U8, "tab_sc")
         nc.vector.memset(tab_sc[:].bitcast(I32), 0)
-        for quad in range(4):
+        for quad in range(P // QUAD):
             nc.sync.dma_start(
-                tab_sc[QUAD * quad : QUAD * quad + 8, :].bitcast(I32),
-                tab_scales[:, 4 * quad : 4 * quad + 4, :].bitcast(I32),
+                tab_sc[QUAD * quad : QUAD * quad + PASSES * SCALE_ROWS, :].bitcast(I32),
+                tab_scales[:, SCALE_ROWS * quad : SCALE_ROWS * (quad + 1), :].bitcast(I32),
             )
-        w_sc_raw = tile([P, H], U8, "w_sc_raw")
-        nc.gpsimd.memset(w_sc_raw[:].bitcast(I32), 0)
+        wad_sc_raw = tile([P, H], U8, "wad_sc_raw")
+        nc.gpsimd.memset(wad_sc_raw[:].bitcast(I32), 0)
 
-        w1_raw = [load_weight(w1[512 * a : 512 * (a + 1), :], "w1_raw%d" % a, "stage%d" % a) for a in range(2)]
+        w1_raw = [
+            load_weight(w1[K_PASS * a : K_PASS * (a + 1), :], "w1_raw%d" % a, "stage%d" % a) for a in range(PASSES)
+        ]
         nc.sync.dma_start(tab[1][:].bitcast(I32), tab_dram[1])
         list2 = load_list(offs2, "list2")
 
@@ -95,21 +103,21 @@ def tile_list_door_drive_sheet_kernel(
         wc_raw = wgs_wc[:, PACK * S :].rearrange("p (i c) -> p i c", i=PACK)
         nc.sync.dma_start(page[0][:], page_rows[0])
         for half in range(2):
-            cols = slice(BANK * half, BANK * (half + 1))
+            cols = slice(HALF * half, HALF * (half + 1))
             load_dealt(wgs_sb[:, 0, cols], wgs, 0, cols)
-        nc.sync.dma_start(page[1][:], page_rows[1])
-        load_dealt(wgs_sb[:, 1, :], wgs, 1, slice(0, S))
-        nc.sync.dma_start(page[2][:], page_rows[2])
-        load_dealt(wgs_sb[:, 2, :], wgs, 2, slice(0, S))
+        for t in (1, 2):
+            nc.sync.dma_start(page[t][:], page_rows[t])
+            load_dealt(wgs_sb[:, t, :], wgs, t, slice(0, S))
 
-        v = [tile([P, S], U32, "v%d" % a) for a in range(2)]
+        v = [tile([P, S], U32, "v%d" % a) for a in range(PASSES)]
         v_sc = tile([P, S], U8, "v_sc")
         nc.vector.tensor_copy(v[0][:], tab[0][:].indirect(list1[:]))
         nc.vector.tensor_copy(v_sc[:], tab_sc[:].indirect(list1[:]))
-        w1_woven = tile([P, 2, PACK * H], BF16, "w1_woven", "woven_weights")
-        round_weight(nc.scalar.copy, w1_raw[0], w1_woven[:, 0, :])
-        round_weight(nc.vector.tensor_copy, w1_raw[1], w1_woven[:, 1, :])
-        w1_q = [quantize(w1_woven[:, a, :], "w1_%d" % a) for a in range(2)]
+        w1_rounded = tile([P, PASSES, PACK * H], BF16, "w1_rounded", "rounded_weights")
+        round_weight(nc.scalar.copy, w1_raw[0], w1_rounded[:, 0, :])
+        round_weight(nc.vector.tensor_copy, w1_raw[1], w1_rounded[:, 1, :])
+        w1_q = [quantize(w1_rounded[:, a, :], "w1_%d" % a) for a in range(PASSES)]
+
         list3 = load_list(offs3, "list3")
         shift_sb = tile([P, PACK], F32, "shift_sb")
         nc.sync.dma_start(shift_sb[:], shift.rearrange("(p t) -> p t", t=PACK))
@@ -120,27 +128,29 @@ def tile_list_door_drive_sheet_kernel(
         nc.sync.dma_start(gm_first[:], gm_rows[:, :, :CHUNK])
         wb_raw = load_weight(wb, "wb_raw", "stage0")
         nc.sync.dma_start(wc_raw, wc.rearrange("(p i) c -> p i c", i=PACK))
+
         for half in range(2):
-            cols = slice(BANK * half, BANK * (half + 1))
-            nc.vector.tensor_copy(v[1][:, cols], tab[1][:].indirect(entries(list1, BANK * half, BANK)))
+            cols = slice(HALF * half, HALF * (half + 1))
+            nc.vector.tensor_copy(v[1][:, cols], tab[1][:].indirect(entries(list1, HALF * half, HALF)))
 
         for t in range(PACK):
             rows = slice(P * t, P * (t + 1))
             h = tile([P, S], F32, "h%d" % t, ("h_even", "h_odd")[t % 2])
             for half in range(2):
-                cols = slice(BANK * half, BANK * (half + 1))
-                h_ps = ps.tile([P, BANK], F32, name="h_ps", tag="h_ps", bufs=2)
-                for a in range(2):
+                cols = slice(HALF * half, HALF * (half + 1))
+                h_ps = ps.tile([P, HALF], F32, name="h_ps", tag="h_ps", bufs=2)
+                for a in range(PASSES):
+                    codes, scales = w1_q[a]
                     nc.tensor.matmul_mx(
                         out=h_ps[:],
-                        lhsT=w1_q[a][0][:, rows].bitcast(FP8X4), lhsT_scale=w1_q[a][1][:, rows],
-                        rhs=v[a][:, cols].bitcast(FP8X4), rhs_scale=v_sc[4 * a : P, cols],
-                        start=(a == 0), stop=(a == 1),
+                        lhsT=codes[:, rows].bitcast(FP8X4), lhsT_scale=scales[:, rows],
+                        rhs=v[a][:, cols].bitcast(FP8X4), rhs_scale=v_sc[SCALE_ROWS * a : P, cols],
+                        start=(a == 0), stop=(a == PASSES - 1),
                     )
                 nc.scalar.copy(h[:, cols], h_ps[:])
                 if t == 0:
                     nc.vector.tensor_tensor(
-                        page[t][:].indirect(entries(list2, BANK * half, BANK)), h[:, cols], wgs_sb[:, t, cols], ALU.mult
+                        page[t][:].indirect(entries(list2, HALF * half, HALF)), h[:, cols], wgs_sb[:, t, cols], ALU.mult
                     )
             if t > 0:
                 nc.vector.tensor_tensor(page[t][:].indirect(list2[:]), h[:], wgs_sb[:, t, :], ALU.mult)
@@ -151,72 +161,73 @@ def tile_list_door_drive_sheet_kernel(
         nc.sync.dma_start(wa_raw[:].bitcast(I32), wa_words[0].bitcast(I32))
         wd_raw = tile([P, H], I32, "wd_raw")
         nc.sync.dma_start(wd_raw[:], wd_words[0].rearrange("p n i -> p (n i)").bitcast(I32))
-        for first, scales in ((0, wa_scales), (4, wd_scales)):
-            for quad in range(4):
+        for first, scales in ((0, wa_scales), (SCALE_ROWS, wd_scales)):
+            for quad in range(P // QUAD):
                 nc.sync.dma_start(
-                    w_sc_raw[QUAD * quad + first : QUAD * quad + first + 4, :].bitcast(I32),
-                    scales[0, 4 * quad : 4 * quad + 4, :].bitcast(I32),
+                    wad_sc_raw[QUAD * quad + first : QUAD * quad + first + SCALE_ROWS, :].bitcast(I32),
+                    scales[0, SCALE_ROWS * quad : SCALE_ROWS * (quad + 1), :].bitcast(I32),
                 )
         list4 = load_list(offs4, "list4")
         cap_sb, wgo_sb = [], []
         for half in range(2):
-            cols = slice(BANK * half, BANK * (half + 1))
-            cap_sb.append(tile([P, PACK, BANK], F32, "cap%d" % half))
+            cols = slice(HALF * half, HALF * (half + 1))
+            cap_sb.append(tile([P, PACK, HALF], F32, "cap%d" % half))
             nc.sync.dma_start(cap_sb[half][:], cap.rearrange("(p t) j -> p t j", t=PACK)[:, :, cols])
-            wgo_sb.append(tile([P, PACK, BANK], F32, "wgo%d" % half))
+            wgo_sb.append(tile([P, PACK, HALF], F32, "wgo%d" % half))
             load_dealt(wgo_sb[half][:], wgo, slice(0, PACK), cols)
 
-        wbc_woven = tile([P, 2, PACK * H], BF16, "wbc_woven", "woven_weights")
-        round_weight(nc.scalar.copy, wb_raw, wbc_woven[:, 0, :])
-        round_weight(nc.scalar.copy, wc_raw, wbc_woven[:, 1, :])
-        x = tile([P, 4, PACK, CHUNK], F32, "x", "wgs_then_x")
-        xg = {}
+        wbc_rounded = tile([P, 2, PACK * H], BF16, "wbc_rounded", "rounded_weights")
+        round_weight(nc.scalar.copy, wb_raw, wbc_rounded[:, 0, :])
+        round_weight(nc.scalar.copy, wc_raw, wbc_rounded[:, 1, :])
+
+        x = tile([P, CHUNKS, PACK, CHUNK], F32, "x", "wgs_then_x")
+        xg, woven, act_q, ya = {}, {}, {}, {}
 
         def pick(chunk):
             for t in range(PACK):
                 nc.vector.tensor_copy(x[:, chunk, t, :], page[t][:].indirect(entries(list3, CHUNK * chunk, CHUNK)))
 
-        def gate(chunk, engine, tag):
-            xg[chunk] = tile([P, PACK, CHUNK], BF16, "xg%d" % chunk, tag)
+        def gate(chunk, engine):
+            xg[chunk] = tile([P, PACK, CHUNK], BF16, "xg%d" % chunk)
             factors = gm_rest[:, :, CHUNK * (chunk - 1) : CHUNK * chunk] if chunk else gm_first[:]
             engine.tensor_tensor(xg[chunk][:], x[:, chunk], factors, ALU.mult)
 
-        woven_tags = ("stage1", "stage0", "woven_third", "woven_last")
-        woven, act_q, ya = {}, {}, {}
-
         def weave(chunk):
-            work = tile([P, 5 * PACK * CHUNK], BF16, "woven_act%d" % chunk, woven_tags[chunk])
-            woven[chunk] = work[:, : 4 * PACK * CHUNK]
-            part = lambda o: work[:, o * PACK * CHUNK : (o + 1) * PACK * CHUNK]
-            xs = part(4).rearrange("p (t j) -> p t j", t=PACK)
+            size = PACK * CHUNK
+            work = tile([P, (OPERANDS + 1) * size], BF16, "woven%d" % chunk, "stage%d" % (1 - chunk % 2))
+            woven[chunk] = work[:, : OPERANDS * size]
+            x_woven, xg_woven, xs_woven, xm_woven, xs_flat = (
+                work[:, o * size : (o + 1) * size] for o in range(OPERANDS + 1)
+            )
+            xs = xs_flat.rearrange("p (t j) -> p t j", t=PACK)
             for t in range(PACK):
                 nc.scalar.activation(xs[:, t, :], x[:, chunk, t, :], ACT.Identity, bias=shift_sb[:, t : t + 1])
 
-            def interleave(o, planes):
+            def interleave(dst, by_tile):
                 nc.scalar.copy(
-                    part(o).rearrange("p (c i t) -> p c t i", i=4, t=PACK),
-                    planes.rearrange("p t (c i) -> p c t i", i=4),
+                    dst.rearrange("p (c i t) -> p c t i", i=LINE, t=PACK),
+                    by_tile.rearrange("p t (c i) -> p c t i", i=LINE),
                 )
 
-            interleave(0, x[:, chunk])
-            interleave(2, xs)
-            nc.scalar.activation(part(3), part(2), ACT.Abs)
-            interleave(1, xg[chunk][:])
+            interleave(x_woven, x[:, chunk])
+            interleave(xs_woven, xs)
+            nc.scalar.activation(xm_woven, xs_woven, ACT.Abs)
+            interleave(xg_woven, xg[chunk][:])
 
         def products(pair, chunk):
             ya_ps = ps.tile([P, 2, CHUNK], F32, name="ya_ps", tag="ya_ps", bufs=3)
             yb_ps = ps.tile([P, 2, CHUNK], F32, name="yb_ps", tag="yb_ps", bufs=3)
+            codes, scales = act_q[chunk]
             for n, t in enumerate((2 * pair, 2 * pair + 1)):
                 rows = slice(P * t, P * (t + 1))
-                rows_c = slice(H + P * t, H + P * (t + 1))
+                rows_wc = slice(H + P * t, H + P * (t + 1))
                 weights = (
-                    (wa_sb[:, 2 * P * t : 2 * P * (t + 1)].bitcast(FP4X4), w_sc[:, rows]),
+                    (wa_sb[:, 2 * P * t : 2 * P * (t + 1)].bitcast(FP4X4), wad_sc[:, rows]),
                     (wbc_codes[:, rows].bitcast(FP8X4), wbc_scales[:, rows]),
-                    (wbc_codes[:, rows_c].bitcast(FP8X4), wbc_scales[:, rows_c]),
-                    (wd_sb[:, rows].bitcast(FP8X4), w_sc[4:P, rows]),
+                    (wbc_codes[:, rows_wc].bitcast(FP8X4), wbc_scales[:, rows_wc]),
+                    (wd_sb[:, rows].bitcast(FP8X4), wad_sc[SCALE_ROWS:P, rows]),
                 )
-                codes, scales = act_q[chunk]
-                for o in range(4):
+                for o in range(OPERANDS):
                     cols = slice(CHUNK * o, CHUNK * (o + 1))
                     nc.tensor.matmul_mx(
                         out=(ya_ps if o < 2 else yb_ps)[:, n, :],
@@ -225,38 +236,45 @@ def tile_list_door_drive_sheet_kernel(
                         start=(o % 2 == 0), stop=(o % 2 == 1),
                     )
             if pair == 0:
-                ya[chunk] = tile([P, PACK, CHUNK], F32, "ya%d" % chunk, ("xg1", "ya_odd", "ya_even", "ya_odd")[chunk])
-            nc.scalar.copy(ya[chunk][:, 2 * pair : 2 * pair + 2, :], ya_ps[:])
-            return ya[chunk][:, 2 * pair : 2 * pair + 2, :], yb_ps
+                ya[chunk] = tile([P, PACK, CHUNK], F32, "ya%d" % chunk, "xg%d" % (chunk + 1))
+            ya_pair = ya[chunk][:, 2 * pair : 2 * pair + 2, :]
+            nc.scalar.copy(ya_pair, ya_ps[:])
+            return ya_pair, yb_ps
 
-        def columns(chunk):
-            return slice(CHUNK * (chunk % 2), CHUNK * (chunk % 2 + 1))
+        def columns(chunk, count=1):
+            return slice(CHUNK * (chunk % 2), CHUNK * (chunk % 2 + count))
 
         def larger(y, pair, chunk):
             ya_pair, yb_ps = products(pair, chunk)
-            nc.vector.tensor_tensor(y[:, 2 * pair : 2 * pair + 2, columns(chunk)], ya_pair, yb_ps[:], ALU.max)
+            nc.vector.tensor_tensor(y[pair][:, :, columns(chunk)], ya_pair, yb_ps[:], ALU.max)
 
         def limit(y, pair, chunk):
-            part = y[:, 2 * pair : 2 * pair + 2, columns(chunk)]
+            part = y[pair][:, :, columns(chunk)]
             nc.vector.tensor_tensor(part, part, cap_sb[chunk // 2][:, 2 * pair : 2 * pair + 2, columns(chunk)], ALU.min)
 
+        def judge(y, chunk):
+            for step in (larger, limit):
+                for pair in range(2):
+                    step(y, pair, chunk)
+
         def rewrite(y, t, chunk, count=1):
-            cols = slice(columns(chunk).start, columns(chunk).start + count * CHUNK)
+            cols = columns(chunk, count)
             nc.vector.tensor_tensor(
                 page[t][:].indirect(entries(list4, CHUNK * chunk, CHUNK * count)),
-                y[:, t, cols], wgo_sb[chunk // 2][:, t, cols], ALU.mult,
+                y[t // 2][:, t % 2, cols], wgo_sb[chunk // 2][:, t, cols], ALU.mult,
             )
 
         def store(t):
             nc.sync.dma_start(out_rows[t], page[t][:])
 
-        for chunk in range(4):
+        for chunk in range(CHUNKS):
             pick(chunk)
-            if chunk < 3:
-                gate(chunk, nc.gpsimd, None)
+            if chunk < CHUNKS - 1:
+                gate(chunk, nc.gpsimd)
             if chunk < 2:
                 weave(chunk)
-        wbc_codes, wbc_scales = quantize(wbc_woven[:].rearrange("p a c -> p (a c)"), "wbc", "h_odd")
+
+        wbc_codes, wbc_scales = quantize(wbc_rounded[:].rearrange("p a c -> p (a c)"), "wbc", "h_odd")
         wa_sb = tile([P, 2 * H], U8, "wa_sb")
         nc.vector.tensor_copy(
             wa_sb[:].bitcast(U16).rearrange("p (t m) -> p t m", t=PACK),
@@ -266,31 +284,31 @@ def tile_list_door_drive_sheet_kernel(
         nc.vector.tensor_copy(
             wd_sb[:].rearrange("p (t m) -> p m t", t=PACK), wd_raw[:].rearrange("p (m t) -> p m t", t=PACK)
         )
-        w_sc = tile([P, H], U8, "w_sc")
+        wad_sc = tile([P, H], U8, "wad_sc")
         nc.vector.tensor_copy(
-            w_sc[:].rearrange("p (t m) -> p t m", t=PACK), w_sc_raw[:].rearrange("p (m t) -> p t m", t=PACK)
+            wad_sc[:].rearrange("p (t m) -> p t m", t=PACK), wad_sc_raw[:].rearrange("p (m t) -> p t m", t=PACK)
         )
+        gate(CHUNKS - 1, nc.vector)
 
         act_q[0] = quantize(woven[0], "act0")
-        gate(3, nc.vector, "stage1")
-        for chunk in range(2):
-            if chunk == 1:
-                weave(2)
-            act_q[chunk + 1] = quantize(woven[chunk + 1], "act%d" % (chunk + 1), (None, "stage0")[chunk])
-            y = tile([P, PACK, BANK], F32, "y%d" % chunk, woven_tags[chunk + 1])
-            for pair in range(2):
-                larger(y, pair, chunk)
-            for pair in range(2):
-                limit(y, pair, chunk)
-            for t in range(PACK):
-                rewrite(y, t, chunk)
+        act_q[1] = quantize(woven[1], "act1")
+        y = [tile([P, 2, HALF], F32, "y0_%d" % pair)[:] for pair in range(2)]
+        judge(y, 0)
+        for t in range(PACK):
+            rewrite(y, t, 0)
+
+        weave(2)
+        act_q[2] = quantize(woven[2], "act2", "y0_0")
+        y1 = tile([P, PACK, HALF], F32, "y1", "y0_1")
+        y = [y1[:, 2 * pair : 2 * pair + 2, :] for pair in range(2)]
+        judge(y, 1)
+        for t in range(PACK):
+            rewrite(y, t, 1)
+
         weave(3)
-        act_q[3] = quantize(woven[3], "act3", "woven_third")
-        y = tile([P, PACK, BANK], F32, "y2", woven_tags[3])
-        for pair in range(2):
-            larger(y, pair, 2)
-        for pair in range(2):
-            limit(y, pair, 2)
+        act_q[3] = quantize(woven[3], "act3", "y0_1")
+        y = [tile([P, 2, HALF], F32, "y2_%d" % pair)[:] for pair in range(2)]
+        judge(y, 2)
         rewrite(y, 0, 2)
         rewrite(y, 1, 2)
         larger(y, 0, 3)
@@ -304,5 +322,5 @@ def tile_list_door_drive_sheet_kernel(
         store(1)
         rewrite(y, 2, 3)
         store(2)
-        rewrite(y, 3, 2, 2)
+        rewrite(y, 3, 2, count=2)
         store(3)

from contextlib import ExitStack

import concourse.mybir as mybir

K, H, T, S, T2, J = 1024, 512, 2048, 1024, 2048, 1024
FLOPS = 2 * K * H * S + 4 * 2 * H * H * J

F32 = mybir.dt.float32
BF16 = mybir.dt.bfloat16
I32 = mybir.dt.int32
U32 = mybir.dt.uint32
U16 = mybir.dt.uint16
U8 = mybir.dt.uint8
FP8X4 = mybir.dt.float8_e4m3fn_x4
FP4X4 = mybir.dt.float4_e2m1fn_x4
ALU = mybir.AluOpType
ACT = mybir.ActivationFunctionType

P = 128
PACK = 4
K_PASS = P * PACK
PASSES = K // K_PASS
QUAD = 32
SCALE_ROWS = 4
STRIPE = 16
HALF = 512
CHUNK = 256
CHUNKS = J // CHUNK
OPERANDS = 4
LINE = 4


def tile_list_door_drive_sheet_kernel(
    tc, tab_words, tab_scales, offs, w1, page0, offs2, wgs, offs3, gm, shift,
    wa_words, wa_scales, wb, wc, wd_words, wd_scales, cap, offs4, wgo, out,
):
    nc = tc.nc
    with ExitStack() as ctx:
        sb = ctx.enter_context(tc.tile_pool(name="sb", bufs=1))
        ps = ctx.enter_context(tc.psum_pool(name="ps", bufs=1))

        def tile(shape, dtype, name, tag=None):
            return sb.tile(shape, dtype, name=name, tag=tag or name, bufs=1, align_bytes=64)

        def load_list(dram, name):
            lst = sb.tile([P, dram.shape[1]], U16, name=name)
            nc.sync.dma_start(lst[:], dram)
            return lst

        def entries(lst, first, count):
            return lst[:, first // STRIPE : (first + count) // STRIPE]

        def load_dealt(dst, factors, slots, cols):
            dealt = factors.rearrange("(q t) j -> q t j", t=PACK)
            for quad in (0, 2, 1, 3):
                nc.sync.dma_start(dst[QUAD * quad : QUAD * (quad + 1)], dealt[:, slots, cols])

        def load_weight(rows, name, tag):
            raw = tile([P, PACK, H], F32, name, tag)
            nc.sync.dma_start(raw[:], rows.rearrange("(p i) c -> p i c", i=PACK))
            return raw[:]

        def round_weight(copy, raw, rounded):
            copy(
                rounded.rearrange("p (t m i) -> p m t i", t=PACK, i=PACK),
                raw.rearrange("p i (m t) -> p m t i", t=PACK),
            )

        def quantize(values, name, tag=None):
            width = values.shape[1] // PACK
            codes = tile([P, width], U32, name + "_codes", tag)
            scales = tile([P, width], U8, name + "_scales")
            nc.vector.quantize_mx(out=codes[:].bitcast(FP8X4), scales=scales[:], in_=values)
            return codes, scales

        page_rows = page0.rearrange("(p t) c -> t p c", t=PACK)
        out_rows = out.rearrange("(p t) c -> t p c", t=PACK)

        list1 = load_list(offs, "list1")
        tab = [tile([P, T], U32, "tab%d" % a) for a in range(PASSES)]
        tab_dram = [tab_words[a].rearrange("p n i -> p (n i)").bitcast(I32) for a in range(PASSES)]
        nc.sync.dma_start(tab[0][:].bitcast(I32), tab_dram[0])

        tab_sc = tile([P, T], U8, "tab_sc")
        nc.vector.memset(tab_sc[:].bitcast(I32), 0)
        for quad in range(P // QUAD):
            nc.sync.dma_start(
                tab_sc[QUAD * quad : QUAD * quad + PASSES * SCALE_ROWS, :].bitcast(I32),
                tab_scales[:, SCALE_ROWS * quad : SCALE_ROWS * (quad + 1), :].bitcast(I32),
            )
        wad_sc_raw = tile([P, H], U8, "wad_sc_raw")
        nc.gpsimd.memset(wad_sc_raw[:].bitcast(I32), 0)

        w1_raw = [
            load_weight(w1[K_PASS * a : K_PASS * (a + 1), :], "w1_raw%d" % a, "stage%d" % a) for a in range(PASSES)
        ]
        nc.sync.dma_start(tab[1][:].bitcast(I32), tab_dram[1])
        list2 = load_list(offs2, "list2")

        page = [tile([P, T2], F32, "page%d" % t) for t in range(PACK)]
        wgs_wc = tile([P, PACK * (S + H)], F32, "wgs_wc", "wgs_then_x")
        wgs_sb = wgs_wc[:, : PACK * S].rearrange("p (t j) -> p t j", t=PACK)
        wc_raw = wgs_wc[:, PACK * S :].rearrange("p (i c) -> p i c", i=PACK)
        nc.sync.dma_start(page[0][:], page_rows[0])
        for half in range(2):
            cols = slice(HALF * half, HALF * (half + 1))
            load_dealt(wgs_sb[:, 0, cols], wgs, 0, cols)
        for t in (1, 2):
            nc.sync.dma_start(page[t][:], page_rows[t])
            load_dealt(wgs_sb[:, t, :], wgs, t, slice(0, S))

        v = [tile([P, S], U32, "v%d" % a) for a in range(PASSES)]
        v_sc = tile([P, S], U8, "v_sc")
        nc.vector.tensor_copy(v[0][:], tab[0][:].indirect(list1[:]))
        nc.vector.tensor_copy(v_sc[:], tab_sc[:].indirect(list1[:]))
        w1_rounded = tile([P, PASSES, PACK * H], BF16, "w1_rounded", "rounded_weights")
        round_weight(nc.scalar.copy, w1_raw[0], w1_rounded[:, 0, :])
        round_weight(nc.vector.tensor_copy, w1_raw[1], w1_rounded[:, 1, :])
        w1_q = [quantize(w1_rounded[:, a, :], "w1_%d" % a) for a in range(PASSES)]

        list3 = load_list(offs3, "list3")
        shift_sb = tile([P, PACK], F32, "shift_sb")
        nc.sync.dma_start(shift_sb[:], shift.rearrange("(p t) -> p t", t=PACK))
        nc.sync.dma_start(page[3][:], page_rows[3])
        load_dealt(wgs_sb[:, 3, :], wgs, 3, slice(0, S))
        gm_rows = gm.rearrange("(p t) j -> p t j", t=PACK)
        gm_first = tile([P, PACK, CHUNK], F32, "gm_first")
        nc.sync.dma_start(gm_first[:], gm_rows[:, :, :CHUNK])
        wb_raw = load_weight(wb, "wb_raw", "stage0")
        nc.sync.dma_start(wc_raw, wc.rearrange("(p i) c -> p i c", i=PACK))

        for half in range(2):
            cols = slice(HALF * half, HALF * (half + 1))
            nc.vector.tensor_copy(v[1][:, cols], tab[1][:].indirect(entries(list1, HALF * half, HALF)))

        for t in range(PACK):
            rows = slice(P * t, P * (t + 1))
            h = tile([P, S], F32, "h%d" % t, ("h_even", "h_odd")[t % 2])
            for half in range(2):
                cols = slice(HALF * half, HALF * (half + 1))
                h_ps = ps.tile([P, HALF], F32, name="h_ps", tag="h_ps", bufs=2)
                for a in range(PASSES):
                    codes, scales = w1_q[a]
                    nc.tensor.matmul_mx(
                        out=h_ps[:],
                        lhsT=codes[:, rows].bitcast(FP8X4), lhsT_scale=scales[:, rows],
                        rhs=v[a][:, cols].bitcast(FP8X4), rhs_scale=v_sc[SCALE_ROWS * a : P, cols],
                        start=(a == 0), stop=(a == PASSES - 1),
                    )
                nc.scalar.copy(h[:, cols], h_ps[:])
                if t == 0:
                    nc.vector.tensor_tensor(
                        page[t][:].indirect(entries(list2, HALF * half, HALF)), h[:, cols], wgs_sb[:, t, cols], ALU.mult
                    )
            if t > 0:
                nc.vector.tensor_tensor(page[t][:].indirect(list2[:]), h[:], wgs_sb[:, t, :], ALU.mult)

        gm_rest = tile([P, PACK, J - CHUNK], F32, "gm_rest")
        nc.sync.dma_start(gm_rest[:], gm_rows[:, :, CHUNK:])
        wa_raw = tile([P, 2 * H], U8, "wa_raw")
        nc.sync.dma_start(wa_raw[:].bitcast(I32), wa_words[0].bitcast(I32))
        wd_raw = tile([P, H], I32, "wd_raw")
        nc.sync.dma_start(wd_raw[:], wd_words[0].rearrange("p n i -> p (n i)").bitcast(I32))
        for first, scales in ((0, wa_scales), (SCALE_ROWS, wd_scales)):
            for quad in range(P // QUAD):
                nc.sync.dma_start(
                    wad_sc_raw[QUAD * quad + first : QUAD * quad + first + SCALE_ROWS, :].bitcast(I32),
                    scales[0, SCALE_ROWS * quad : SCALE_ROWS * (quad + 1), :].bitcast(I32),
                )
        list4 = load_list(offs4, "list4")
        cap_sb, wgo_sb = [], []
        for half in range(2):
            cols = slice(HALF * half, HALF * (half + 1))
            cap_sb.append(tile([P, PACK, HALF], F32, "cap%d" % half))
            nc.sync.dma_start(cap_sb[half][:], cap.rearrange("(p t) j -> p t j", t=PACK)[:, :, cols])
            wgo_sb.append(tile([P, PACK, HALF], F32, "wgo%d" % half))
            load_dealt(wgo_sb[half][:], wgo, slice(0, PACK), cols)

        wbc_rounded = tile([P, 2, PACK * H], BF16, "wbc_rounded", "rounded_weights")
        round_weight(nc.scalar.copy, wb_raw, wbc_rounded[:, 0, :])
        round_weight(nc.scalar.copy, wc_raw, wbc_rounded[:, 1, :])

        x = tile([P, CHUNKS, PACK, CHUNK], F32, "x", "wgs_then_x")
        xg, woven, act_q, ya = {}, {}, {}, {}

        def pick(chunk):
            for t in range(PACK):
                nc.vector.tensor_copy(x[:, chunk, t, :], page[t][:].indirect(entries(list3, CHUNK * chunk, CHUNK)))

        def gate(chunk, engine):
            xg[chunk] = tile([P, PACK, CHUNK], BF16, "xg%d" % chunk)
            factors = gm_rest[:, :, CHUNK * (chunk - 1) : CHUNK * chunk] if chunk else gm_first[:]
            engine.tensor_tensor(xg[chunk][:], x[:, chunk], factors, ALU.mult)

        def weave(chunk):
            size = PACK * CHUNK
            work = tile([P, (OPERANDS + 1) * size], BF16, "woven%d" % chunk, "stage%d" % (1 - chunk % 2))
            woven[chunk] = work[:, : OPERANDS * size]
            x_woven, xg_woven, xs_woven, xm_woven, xs_flat = (
                work[:, o * size : (o + 1) * size] for o in range(OPERANDS + 1)
            )
            xs = xs_flat.rearrange("p (t j) -> p t j", t=PACK)
            for t in range(PACK):
                nc.scalar.activation(xs[:, t, :], x[:, chunk, t, :], ACT.Identity, bias=shift_sb[:, t : t + 1])

            def interleave(dst, by_tile):
                nc.scalar.copy(
                    dst.rearrange("p (c i t) -> p c t i", i=LINE, t=PACK),
                    by_tile.rearrange("p t (c i) -> p c t i", i=LINE),
                )

            interleave(x_woven, x[:, chunk])
            interleave(xs_woven, xs)
            nc.scalar.activation(xm_woven, xs_woven, ACT.Abs)
            interleave(xg_woven, xg[chunk][:])

        def products(pair, chunk):
            ya_ps = ps.tile([P, 2, CHUNK], F32, name="ya_ps", tag="ya_ps", bufs=3)
            yb_ps = ps.tile([P, 2, CHUNK], F32, name="yb_ps", tag="yb_ps", bufs=3)
            codes, scales = act_q[chunk]
            for n, t in enumerate((2 * pair, 2 * pair + 1)):
                rows = slice(P * t, P * (t + 1))
                rows_wc = slice(H + P * t, H + P * (t + 1))
                weights = (
                    (wa_sb[:, 2 * P * t : 2 * P * (t + 1)].bitcast(FP4X4), wad_sc[:, rows]),
                    (wbc_codes[:, rows].bitcast(FP8X4), wbc_scales[:, rows]),
                    (wbc_codes[:, rows_wc].bitcast(FP8X4), wbc_scales[:, rows_wc]),
                    (wd_sb[:, rows].bitcast(FP8X4), wad_sc[SCALE_ROWS:P, rows]),
                )
                for o in range(OPERANDS):
                    cols = slice(CHUNK * o, CHUNK * (o + 1))
                    nc.tensor.matmul_mx(
                        out=(ya_ps if o < 2 else yb_ps)[:, n, :],
                        lhsT=weights[o][0], lhsT_scale=weights[o][1],
                        rhs=codes[:, cols].bitcast(FP8X4), rhs_scale=scales[:, cols],
                        start=(o % 2 == 0), stop=(o % 2 == 1),
                    )
            if pair == 0:
                ya[chunk] = tile([P, PACK, CHUNK], F32, "ya%d" % chunk, "xg%d" % (chunk + 1))
            ya_pair = ya[chunk][:, 2 * pair : 2 * pair + 2, :]
            nc.scalar.copy(ya_pair, ya_ps[:])
            return ya_pair, yb_ps

        def columns(chunk, count=1):
            return slice(CHUNK * (chunk % 2), CHUNK * (chunk % 2 + count))

        def larger(y, pair, chunk):
            ya_pair, yb_ps = products(pair, chunk)
            nc.vector.tensor_tensor(y[pair][:, :, columns(chunk)], ya_pair, yb_ps[:], ALU.max)

        def limit(y, pair, chunk):
            part = y[pair][:, :, columns(chunk)]
            nc.vector.tensor_tensor(part, part, cap_sb[chunk // 2][:, 2 * pair : 2 * pair + 2, columns(chunk)], ALU.min)

        def judge(y, chunk):
            for step in (larger, limit):
                for pair in range(2):
                    step(y, pair, chunk)

        def rewrite(y, t, chunk, count=1):
            cols = columns(chunk, count)
            nc.vector.tensor_tensor(
                page[t][:].indirect(entries(list4, CHUNK * chunk, CHUNK * count)),
                y[t // 2][:, t % 2, cols], wgo_sb[chunk // 2][:, t, cols], ALU.mult,
            )

        def store(t):
            nc.sync.dma_start(out_rows[t], page[t][:])

        for chunk in range(CHUNKS):
            pick(chunk)
            if chunk < CHUNKS - 1:
                gate(chunk, nc.gpsimd)
            if chunk < 2:
                weave(chunk)

        wbc_codes, wbc_scales = quantize(wbc_rounded[:].rearrange("p a c -> p (a c)"), "wbc", "h_odd")
        wa_sb = tile([P, 2 * H], U8, "wa_sb")
        nc.vector.tensor_copy(
            wa_sb[:].bitcast(U16).rearrange("p (t m) -> p t m", t=PACK),
            wa_raw[:].bitcast(U16).rearrange("p (m t) -> p t m", t=PACK),
        )
        wd_sb = tile([P, H], I32, "wd_sb")
        nc.vector.tensor_copy(
            wd_sb[:].rearrange("p (t m) -> p m t", t=PACK), wd_raw[:].rearrange("p (m t) -> p m t", t=PACK)
        )
        wad_sc = tile([P, H], U8, "wad_sc")
        nc.vector.tensor_copy(
            wad_sc[:].rearrange("p (t m) -> p t m", t=PACK), wad_sc_raw[:].rearrange("p (m t) -> p t m", t=PACK)
        )
        gate(CHUNKS - 1, nc.vector)

        act_q[0] = quantize(woven[0], "act0")
        act_q[1] = quantize(woven[1], "act1")
        y = [tile([P, 2, HALF], F32, "y0_%d" % pair)[:] for pair in range(2)]
        judge(y, 0)
        for t in range(PACK):
            rewrite(y, t, 0)

        weave(2)
        act_q[2] = quantize(woven[2], "act2", "y0_0")
        y1 = tile([P, PACK, HALF], F32, "y1", "y0_1")
        y = [y1[:, 2 * pair : 2 * pair + 2, :] for pair in range(2)]
        judge(y, 1)
        for t in range(PACK):
            rewrite(y, t, 1)

        weave(3)
        act_q[3] = quantize(woven[3], "act3", "y0_1")
        y = [tile([P, 2, HALF], F32, "y2_%d" % pair)[:] for pair in range(2)]
        judge(y, 2)
        rewrite(y, 0, 2)
        rewrite(y, 1, 2)
        larger(y, 0, 3)
        rewrite(y, 2, 2)
        limit(y, 0, 3)
        larger(y, 1, 3)
        rewrite(y, 0, 3)
        store(0)
        limit(y, 1, 3)
        rewrite(y, 1, 3)
        store(1)
        rewrite(y, 2, 3)
        store(2)
        rewrite(y, 3, 2, count=2)
        store(3)
